import numpy as np
CORES = [13,29,45,61,77,93,109]
N = 7
KT, F = 1, 64
def setup_inputs(rng):
    return {"a": rng.standard_normal((N, 128, KT * 128), dtype=np.float32), "w": rng.standard_normal((N, 128, KT * F), dtype=np.float32)}
def reference(a, w):
    tot = np.zeros((128, F))
    for j in range(N):
        for t in range(KT):
            tot += a[j][:, 128 * t:128 * t + 128].astype(np.float64).T @ w[j][:, F * t:F * t + F].astype(np.float64)
    tot = np.maximum(tot, 0.0)
    s = tot.astype(np.float32 if a.dtype != np.float64 else np.float64)
    return {"y": np.broadcast_to(s, (N,) + s.shape)}

from concourse.bass import DstId, RemoteDMATransfer
from concourse.mybir import AluOpType

N = 7
F = 64

SCRATCH = {
    "a_sb": ("sbuf", [128, 128], "float32"),
    "w_sb": ("sbuf", [128, F], "float32"),
    "p_sb": ("sbuf", [128, F], "float32"),
    "land": ("sbuf", [128, N * F], "float32"),
    "zero": ("sbuf", [128, F], "float32"),
    "y_sb": ("sbuf", [128, F], "float32"),
    "ps": ("psum", [128, F], "float32"),
}
SEMAPHORES = ["ld", "zs", "mm", "cp", "sent", "acc", "fin", "st"] + ["arr%d" % j for j in range(N)]


def _bits(m):
    return bin(m).count("1")


def rank_program(g, core, T, topo):
    rank = T.rank_of(core)
    if rank is None:
        return
    S = T.sem
    cores = T.cores

    g.sync.dma_start(T.a_sb[:], T.a[:]).then_inc(S.ld, 16)
    g.scalar.dma_start(T.w_sb[:], T.w[:]).then_inc(S.ld, 16)
    g.vector.memset(T.zero[:], 0.0).then_inc(S.zs, 1)

    g.tensor.wait_ge(S.ld, 32)
    g.tensor.matmul(T.ps[:], T.a_sb[:], T.w_sb[:], True, True).then_inc(S.mm, 1)
    g.vector.wait_ge(S.mm, 1)
    g.vector.tensor_copy(T.p_sb[:], T.ps[:]).then_inc(S.cp, 1)

    peers = [cores[(rank + k) % N] for k in range(1, N)]
    mask = 0xFFFF
    for d in peers:
        mask &= topo.mask(core, d)
    ne = _bits(mask)
    slot = T.land[:, rank * F:(rank + 1) * F]
    ids = []
    for d in peers:
        rid, pid, _se = topo.addr(d)
        ids.append(DstId(rid=rid, pnc=pid))
    g.wait_ge(S.cp, 1)
    g.remote_dma_fused(
        [RemoteDMATransfer(dst_ids=ids, dma_engine_mask=mask, remote_sem=S["arr%d" % rank],
                           srcs=[T.p_sb[:]], dsts=[slot for _ in peers], alu_op=0)],
        local_sem=S.sent)

    g.vector.wait_ge(S.cp, 1)
    for k in range(1, N):
        src = (rank - k) % N
        g.vector.wait_ge(S["arr%d" % src], _bits(topo.mask(cores[src], core)))
        if k > 1:
            g.vector.wait_ge(S.acc, k - 1)
        g.vector.tensor_tensor(T.ps[:], T.ps[:], T.land[:, src * F:(src + 1) * F], AluOpType.add).then_inc(S.acc, 1)
    g.vector.wait_ge(S.acc, N - 1)
    g.vector.wait_ge(S.zs, 1)
    g.vector.tensor_tensor(T.y_sb[:], T.ps[:], T.zero[:], AluOpType.max).then_inc(S.fin, 1)

    g.sync.wait_ge(S.fin, 1)
    g.sync.dma_start(T.y[:], T.y_sb[:]).then_inc(S.st, 16)
    g.sync.wait_ge(S.st, 16)
    g.wait_ge(S.sent, ne)
